import numpy as np
import ml_dtypes


def mxq(x, axis, fmt="e4m3"):
    dtype, down = {"e4m3": (ml_dtypes.float8_e4m3fn, 7), "e5m2": (ml_dtypes.float8_e5m2, 14)}[fmt]
    v = np.moveaxis(np.asarray(x, np.float32).astype(ml_dtypes.bfloat16).astype(np.float64), axis, -1)
    blocks = v.reshape(v.shape[:-1] + (-1, 32))
    amax = np.abs(blocks).max(-1, keepdims=True)
    byte = np.maximum(np.where(amax > 0, np.frexp(amax)[1] - 1 + 127, 0) - down, 1)
    scale = np.exp2(byte - 127.0)
    codes = (blocks / scale).astype(np.float32).astype(dtype).astype(np.float64)
    return np.moveaxis((codes * scale).reshape(v.shape), -1, axis)


WIDE = False


def mx_kscale(k):
    if not WIDE:
        return np.ones(k)
    levels = np.array([10, -10, 5, -5, 0])
    if k % 512:
        return np.exp2(np.random.permutation(np.resize(levels, k // 32))).repeat(32)
    a = np.empty((k // 512, 16))
    for p in range(k // 512):
        a[p, :8] = np.random.permutation(np.resize(levels, 8))
        for g in range(8):
            far = levels[np.abs(levels - a[p, g]) >= 10]
            a[p, g + 8] = far[np.random.randint(len(far))]
    return np.exp2(a.ravel()).repeat(32)


def f64(x):
    return np.asarray(x).astype(np.float64)


def striped(idx):
    return np.tile(idx.reshape(-1, 16).T, (8, 1)).astype(np.uint16)


def unstriped(offs):
    return offs[:16].T.reshape(-1).astype(np.int64)


def pack_weight(w):
    k, n = w.shape
    w = f64(np.asarray(w, np.float32).astype(ml_dtypes.bfloat16)).reshape(k // 32, 32, n)
    amax = np.abs(w).max(1)
    byte = np.clip(np.where(amax > 0, np.frexp(amax)[1] - 1 + 127 - 7, 1), 1, 254)
    scaled = (w * np.exp2(127.0 - byte)[:, None, :]).reshape(k, n).astype(np.float32)
    words = np.ascontiguousarray(scaled.reshape(k // 512, 128, 4, n).transpose(0, 1, 3, 2)).astype(ml_dtypes.float8_e4m3fn).view(np.uint8)
    return words, np.ascontiguousarray(byte.astype(np.uint8).reshape(k // 512, 16, n))


def unpack_weight(words, scales):
    g, p, n, _ = words.shape
    vals = np.ascontiguousarray(words).view(ml_dtypes.float8_e4m3fn).astype(np.float64) * np.repeat(np.exp2(scales.astype(np.float64) - 127.0), 8, axis=1)[..., None]
    return vals.transpose(0, 1, 3, 2).reshape(g * 512, n)


E2M1 = np.array([0.0, 0.5, 1.0, 1.5, 2.0, 3.0, 4.0, 6.0, -0.0, -0.5, -1.0, -1.5, -2.0, -3.0, -4.0, -6.0])


def pack_fp4(w):
    k, n = w.shape
    w = f64(np.asarray(w, np.float32).astype(ml_dtypes.bfloat16)).reshape(k // 32, 32, n)
    amax = np.abs(w).max(1)
    mant, ex = np.frexp(amax / 6.0)
    byte = np.clip(np.where(amax > 0, np.where(mant > 0.5, ex, ex - 1) + 127, 1), 1, 254)
    scaled = (w * np.exp2(127.0 - byte)[:, None, :]).reshape(k, n).astype(np.float32)
    c = np.ascontiguousarray(scaled.reshape(k // 512, 128, 4, n).transpose(0, 1, 3, 2)).astype(ml_dtypes.float4_e2m1fn).view(np.uint8) & 0xF
    words = (c[..., 0::2] | (c[..., 1::2] << 4)).reshape(k // 512, 128, 2 * n)
    return np.ascontiguousarray(words), np.ascontiguousarray(byte.astype(np.uint8).reshape(k // 512, 16, n))


def unpack_fp4(words, scales):
    g, _, n = scales.shape
    words = np.ascontiguousarray(words).reshape(g, 128, n, 2)
    nib = np.empty((g, 128, n, 4), np.uint8)
    nib[..., 0::2] = words & 0xF
    nib[..., 1::2] = words >> 4
    vals = E2M1[nib] * np.repeat(np.exp2(scales.astype(np.float64) - 127.0), 8, axis=1)[..., None]
    return vals.transpose(0, 1, 3, 2).reshape(g * 512, n)


K, T, S, D, N, H, V, U = 512, 4096, 1024, 4, 256, 512, 256, 512


def setup_inputs():
    n = np.random.standard_normal
    s = mx_kscale(K)[:, None]
    u = mx_kscale(H)
    packed_xT = pack_weight(n((K, T)) * s)
    packed_w1 = pack_fp4(n((K, H)) / np.sqrt(K) / s)
    packed_w2 = pack_fp4(n((H, N)) / np.sqrt(H) / u[:, None])
    return {
        "x_words": packed_xT[0],
        "x_scales": packed_xT[1],
        "w1_words": packed_w1[0],
        "w1_scales": packed_w1[1],
        "st": (np.random.uniform(0.6, 1.4, (H, S))).astype(np.float32),
        "mod": (0.5 * n((H, U))).astype(np.float32),
        "unit": (np.random.uniform(0.6, 1.4, (H, 1)) * u[:, None]).astype(np.float32),
        "w2_words": packed_w2[0],
        "w2_scales": packed_w2[1],
        "offs": striped(np.random.permutation(T)[:S]),
        "mv": striped(np.random.permutation(S)),
        "out_t": striped(np.random.permutation(np.concatenate([np.arange(V), np.random.randint(0, V, U - V)]))),
    }


def reference(x_words, x_scales, w1_words, w1_scales, st, mod, unit, w2_words, w2_scales, offs, mv, out_t):
    xq = unpack_weight(x_words, x_scales)[:, unstriped(offs)]
    y = unpack_fp4(w1_words, w1_scales).T @ xq
    ym = y[:, unstriped(mv)]
    flat = ym * f64(st)
    stack = flat.reshape(len(flat), -1, D).sum(axis=2)
    t2 = (flat) ** 2
    energ = t2.reshape(len(t2), -1, D).sum(axis=2)
    semb = ((stack) ** 2) / (4.0 * energ + 0.5)
    sbu = semb[:, unstriped(out_t)]
    wst = stack[:, unstriped(out_t)] * sbu
    hid = f64(unit) * (wst - f64(mod))
    return unpack_fp4(w2_words, w2_scales).T @ mxq(hid, 0, "e4m3")

@@ -1,0 +1,242 @@
+from contextlib import ExitStack
+
+import concourse.mybir as mybir
+from concourse.masks import make_identity
+
+K, T, S, D, N, H, V, U = 512, 4096, 1024, 4, 256, 512, 256, 512
+FLOPS = 2 * K * H * S + 2 * H * N * U
+
+F32 = mybir.dt.float32
+BF16 = mybir.dt.bfloat16
+I32 = mybir.dt.int32
+U32 = mybir.dt.uint32
+U16 = mybir.dt.uint16
+U8 = mybir.dt.uint8
+FP8X4 = mybir.dt.float8_e4m3fn_x4
+FP4X4 = mybir.dt.float4_e2m1fn_x4
+ALU = mybir.AluOpType
+ACT = mybir.ActivationFunctionType
+
+P = 128
+PACK = 4
+HALF = 512
+VB = 128
+RH = 256
+FUSED = (1, 2, 3)
+PAIRED = (2, 3)
+
+
+def load_scale_rows(queues, plane, rows):
+    for q, queue in enumerate(queues):
+        queue.dma_start(out=plane[32 * q : 32 * q + 4, :].bitcast(I32), in_=rows[0, 4 * q : 4 * q + 4, :].bitcast(I32))
+
+
+def tile_picked_ysembl_mul_p_kernel(
+    tc, x_words, x_scales, w1_words, w1_scales, st, mod, unit, w2_words, w2_scales, offs, mv, out_t, out
+):
+    nc = tc.nc
+    with ExitStack() as ctx:
+        keep = ctx.enter_context(tc.tile_pool(name="keep", bufs=1))
+        psum_y = ctx.enter_context(tc.psum_pool(name="psum_y", bufs=4))
+        psum_sum = ctx.enter_context(tc.psum_pool(name="psum_sum", bufs=4))
+
+        def sb(name, shape, dtype, tag=None):
+            return keep.tile(shape, dtype, name=name, tag=tag or name, align_bytes=64)
+
+        offs_sb = keep.tile([P, S // 16], U16, name="offs_sb")
+        mv_sb = keep.tile([P, S // 16], U16, name="mv_sb")
+        out_t_sb = keep.tile([P, U // 16], U16, name="out_t_sb")
+
+        x_table = sb("x_table", [P, T], I32)
+        xs_table = sb("xs_table", [P, T], U8)
+        w1_raw = sb("w1_raw", [P, 2 * H], U8)
+        w1s_raw = sb("w1s_raw", [P, H], U8)
+        w2_sb = sb("w2_sb", [P, 2 * N], U8)
+        w2s_sb = sb("w2s_sb", [P, N], U8)
+        unit_sb = sb("unit_sb", [P, PACK], F32)
+        ident = sb("ident", [P, P], F32)
+
+        st_rows = st.rearrange("(p t) j -> t p j", t=PACK)
+        mod_rows = mod.rearrange("(p t) r -> p t r", t=PACK)
+        mod_early = sb("mod_early", [P, PACK - 1, U], F32)
+        nc.vector.memset(xs_table[:].bitcast(I32), 0)
+        nc.gpsimd.memset(w1s_raw[:].bitcast(I32), 0)
+        nc.gpsimd.memset(w2s_sb[:].bitcast(I32), 0)
+        load_scale_rows([nc.scalar] * 4, xs_table, x_scales)
+        load_scale_rows([nc.gpsimd, nc.gpsimd, nc.scalar, nc.scalar], w1s_raw, w1_scales)
+        nc.sync.dma_start(offs_sb[:], offs)
+        nc.sync.dma_start(out=w1_raw[:].bitcast(I32), in_=w1_words[0].bitcast(I32))
+        nc.sync.dma_start(mv_sb[:], mv)
+        nc.sync.dma_start(out_t_sb[:], out_t)
+        nc.sync.dma_start(out=x_table[:], in_=x_words[0].rearrange("p c r -> p (c r)").bitcast(I32))
+        nc.sync.dma_start(out=mod_early[:], in_=mod_rows[:, 1:, :])
+        nc.gpsimd.dma_start(out=unit_sb[:], in_=unit.rearrange("(p t) o -> p (t o)", t=PACK))
+        make_identity(nc, ident[:])
+        nc.gpsimd.dma_start(out=w2_sb[:].bitcast(I32), in_=w2_words[0].bitcast(I32))
+        load_scale_rows([nc.gpsimd] * 4, w2s_sb, w2_scales)
+
+        w1_dealt = sb("w1_dealt", [P, 2 * H], U8)
+        w1s_dealt = sb("w1s_dealt", [P, H], U8)
+        nc.vector.tensor_copy(
+            out=w1_dealt[:].rearrange("p (t m b) -> p m t b", t=PACK, b=2),
+            in_=w1_raw[:].rearrange("p (m t b) -> p m t b", t=PACK, b=2),
+        )
+        nc.vector.tensor_copy(
+            out=w1s_dealt[:].rearrange("p (t m) -> p m t", t=PACK),
+            in_=w1s_raw[:].rearrange("p (m t) -> p m t", t=PACK),
+        )
+
+        xs_picked = sb("xs_picked", [P, S], U8)
+        nc.vector.tensor_copy(xs_picked[:], xs_table[:].indirect(offs_sb[:]))
+        x_both = sb("x_picked", [P, S], U32, tag="xs_table")
+        x_picked = [x_both[:, HALF * h : HALF * (h + 1)] for h in range(2)]
+        for h in range(2):
+            nc.vector.tensor_copy(x_picked[h], x_table[:].bitcast(U32).indirect(offs_sb[:, 32 * h : 32 * (h + 1)]))
+
+        late = sb("late", [P, 3 * S + U], F32, tag="x_table")
+        st_sb = [sb("st0", [P, S], F32, tag="w1_raw")] + [late[:, S * t : S * (t + 1)] for t in range(PACK - 1)]
+        mod_first = late[:, 3 * S :]
+        for t in range(PACK):
+            nc.sync.dma_start(out=st_sb[t][:, :], in_=st_rows[t])
+        nc.sync.dma_start(out=mod_first, in_=mod_rows[:, 0, :])
+
+        y_sb = [sb(f"y{t}", [P, S], F32) for t in range(PACK)]
+        flat = [[sb(f"flat{t}_{h}", [P, HALF], F32) for h in range(2)] for t in range(PACK)]
+        sq = [[sb(f"sq{t}_{h}", [P, D, VB], F32) for h in range(2)] for t in range(PACK)]
+        win = [sb(f"win{t}", [P, 3, V], F32) for t in range(PACK)]
+        semb = [sb(f"semb{t}", [P, V], F32)[:, :] for t in range(PACK)]
+        rsq = [sb(f"rsq{t}", [P, V], F32)[:, :] for t in range(PACK)]
+        picked = [sb(f"picked{t}", [P, U], F32) for t in range(PACK)]
+        hid32 = [sb(f"hid32_{r}", [P, PACK, RH], F32) for r in range(2)]
+        neg_unit = sb("neg_unit", [P, PACK], F32)
+        sums = {}
+
+        def first_product(t):
+            for h in range(2):
+                bank = psum_y.tile([P, HALF], F32, name="bank")
+                nc.tensor.matmul_mx(
+                    out=bank[:],
+                    lhsT=w1_dealt[:, 2 * P * t : 2 * P * (t + 1)].bitcast(FP4X4),
+                    lhsT_scale=w1s_dealt[:, P * t : P * (t + 1)],
+                    rhs=x_picked[h].bitcast(FP8X4),
+                    rhs_scale=xs_picked[:, HALF * h : HALF * (h + 1)],
+                    start=True,
+                    stop=True,
+                )
+                dst = y_sb[t][:, HALF * h : HALF * (h + 1)]
+                if t == 0 and h == 1:
+                    nc.vector.tensor_copy(out=dst, in_=bank[:])
+                else:
+                    nc.scalar.copy(out=dst, in_=bank[:])
+
+        def moveout(t, h):
+            if h == 0:
+                sums[t] = psum_sum.tile([P, 2, V], F32, name="sums")
+            nc.vector.tensor_tensor(
+                flat[t][h][:],
+                y_sb[t][:].indirect(mv_sb[:, 32 * h : 32 * (h + 1)]),
+                st_sb[t][:, HALF * h : HALF * (h + 1)],
+                ALU.mult,
+            )
+            nc.scalar.activation(
+                out=sq[t][h][:].rearrange("p d v -> p v d"),
+                in_=flat[t][h][:].rearrange("p (v d) -> p v d", d=D),
+                func=ACT.Square,
+            )
+            if t in PAIRED:
+                pairs = sb(f"pairs{t}_{h}", [P, VB, 2], F32)
+                groups = flat[t][h][:].rearrange("p (v d) -> p v d", d=D)
+                nc.vector.tensor_tensor(pairs[:], groups[:, :, 0:2], groups[:, :, 2:4], ALU.add)
+                terms = [pairs[:, :, e] for e in range(2)]
+            else:
+                terms = [flat[t][h][:, d::D] for d in range(D)]
+            cols = slice(VB * h, VB * (h + 1))
+            for a, planes in enumerate((terms, [sq[t][h][:, d, :] for d in range(D)])):
+                for n, plane in enumerate(planes):
+                    nc.tensor.matmul(
+                        sums[t][:, a, cols], lhsT=plane, rhs=ident[:],
+                        start=(n == 0), stop=(n == len(planes) - 1), is_transpose=True,
+                    )
+
+        def ratio(t):
+            stack, energ = sums[t][:, 0, :], sums[t][:, 1, :]
+            rs, q = rsq[t], win[t][:, 1, :]
+            nc.scalar.activation(out=rs, in_=energ, func=ACT.Abs_reciprocal_sqrt, scale=4.0, bias=0.5)
+            nc.vector.tensor_tensor(q, stack, rs, ALU.mult)
+
+        def weighted(t):
+            stack, q, w = sums[t][:, 0, :], win[t][:, 1, :], win[t][:, 2, :]
+            nc.scalar.activation(out=semb[t], in_=q, func=ACT.Square)
+            nc.vector.tensor_tensor(w, stack, semb[t], ALU.mult)
+            back = psum_y.tile([P, HALF], F32, name="bank")
+            for h in range(2):
+                cols = slice(VB * h, VB * (h + 1))
+                nc.tensor.transpose(back[:, cols], win[t][:, 2, cols], ident[:])
+            nc.scalar.activation(out=win[t][:, 0, :], in_=back[:, :V], func=ACT.Copy, scale=unit_sb[:, t : t + 1])
+
+        def output_times(t):
+            window = win[t][:].rearrange("p a v -> p (a v)")
+            if t in FUSED:
+                for r in range(2):
+                    nc.vector.tensor_tensor(
+                        hid32[r][:, t, :],
+                        window.indirect(out_t_sb[:, 16 * r : 16 * (r + 1)]),
+                        picked[t][:, RH * r : RH * (r + 1)],
+                        ALU.subtract,
+                    )
+            else:
+                nc.scalar.activation(picked[t][:], window.indirect(out_t_sb[:]), ACT.Copy)
+                for r in range(2):
+                    cols = slice(RH * r, RH * (r + 1))
+                    nc.vector.scalar_tensor_tensor(
+                        hid32[r][:, t, :], mod_first[:, cols], neg_unit[:, t : t + 1], picked[t][:, cols],
+                        ALU.mult, ALU.add,
+                    )
+
+        nc.vector.tensor_scalar(neg_unit[:], unit_sb[:], -1.0, None, ALU.mult)
+        for t in FUSED:
+            nc.scalar.activation(out=picked[t][:], in_=mod_early[:, t - 1, :], func=ACT.Copy, scale=unit_sb[:, t : t + 1])
+        first_product(0)
+        first_product(1)
+        moveout(0, 0)
+        moveout(0, 1)
+        first_product(2)
+        moveout(1, 0)
+        first_product(3)
+        moveout(1, 1)
+        for t in (2, 3):
+            for h in range(2):
+                moveout(t, h)
+        for t in range(PACK):
+            ratio(t)
+            weighted(t)
+        for t in range(PACK):
+            output_times(t)
+
+        out_rows = out.rearrange("(b p) r -> p b r", p=P)
+        for r in range(2):
+            hid = sb(f"hid{r}", [P, RH, PACK], BF16)
+            (nc.scalar.copy if r == 0 else nc.vector.tensor_copy)(
+                out=hid[:].rearrange("p (c i) t -> p c t i", i=4),
+                in_=hid32[r][:].rearrange("p t (c i) -> p c t i", i=4),
+            )
+            codes = sb(f"codes{r}", [P, RH], U32)
+            scales = sb(f"scales{r}", [P, RH], U8)
+            nc.vector.quantize_mx(out=codes[:].bitcast(FP8X4), scales=scales[:], in_=hid[:].rearrange("p r t -> p (r t)"))
+            result = sb(f"result{r}", [P, N // P, RH], F32)
+            for b in range(N // P):
+                bank = psum_y.tile([P, HALF], F32, name="bank")
+                nc.tensor.matmul_mx(
+                    out=bank[:, :RH],
+                    lhsT=w2_sb[:, 2 * P * b : 2 * P * (b + 1)].bitcast(FP4X4),
+                    lhsT_scale=w2s_sb[:, P * b : P * (b + 1)],
+                    rhs=codes[:].bitcast(FP8X4),
+                    rhs_scale=scales[:],
+                    start=True,
+                    stop=True,
+                )
+                if r == 1 and b == 1:
+                    nc.vector.tensor_copy(out=result[:, b, :], in_=bank[:, :RH])
+                else:
+                    nc.scalar.copy(out=result[:, b, :], in_=bank[:, :RH])
+            nc.sync.dma_start(out=out_rows[:, :, RH * r : RH * (r + 1)], in_=result[:])

@@ -22,8 +22,7 @@ PACK = 4
 HALF = 512
 VB = 128
 RH = 256
-FUSED = (1, 2, 3)
-PAIRED = (2, 3)
+FUSED = (3,)
 
 
 def load_scale_rows(queues, plane, rows):
@@ -37,6 +36,7 @@ def tile_picked_ysembl_mul_p_kernel(
     nc = tc.nc
     with ExitStack() as ctx:
         keep = ctx.enter_context(tc.tile_pool(name="keep", bufs=1))
+        ring = ctx.enter_context(tc.tile_pool(name="ring", bufs=3))
         psum_y = ctx.enter_context(tc.psum_pool(name="psum_y", bufs=4))
         psum_sum = ctx.enter_context(tc.psum_pool(name="psum_sum", bufs=4))
 
@@ -57,33 +57,34 @@ def tile_picked_ysembl_mul_p_kernel(
         ident = sb("ident", [P, P], F32)
 
         st_rows = st.rearrange("(p t) j -> t p j", t=PACK)
-        mod_rows = mod.rearrange("(p t) r -> p t r", t=PACK)
-        mod_early = sb("mod_early", [P, PACK - 1, U], F32)
+        warm = sb("warm", [P, 2], F32)
+        nc.gpsimd.memset(warm[:, 0:1], 1.0)
+        nc.scalar.activation(out=warm[:, 1:2], in_=warm[:, 0:1], func=ACT.Abs_reciprocal_sqrt, scale=4.0, bias=0.5)
+
         nc.vector.memset(xs_table[:].bitcast(I32), 0)
-        nc.gpsimd.memset(w1s_raw[:].bitcast(I32), 0)
-        nc.gpsimd.memset(w2s_sb[:].bitcast(I32), 0)
-        load_scale_rows([nc.scalar] * 4, xs_table, x_scales)
-        load_scale_rows([nc.gpsimd, nc.gpsimd, nc.scalar, nc.scalar], w1s_raw, w1_scales)
+        nc.vector.memset(w1s_raw[:].bitcast(I32), 0)
         nc.sync.dma_start(offs_sb[:], offs)
-        nc.sync.dma_start(out=w1_raw[:].bitcast(I32), in_=w1_words[0].bitcast(I32))
         nc.sync.dma_start(mv_sb[:], mv)
         nc.sync.dma_start(out_t_sb[:], out_t)
         nc.sync.dma_start(out=x_table[:], in_=x_words[0].rearrange("p c r -> p (c r)").bitcast(I32))
-        nc.sync.dma_start(out=mod_early[:], in_=mod_rows[:, 1:, :])
-        nc.gpsimd.dma_start(out=unit_sb[:], in_=unit.rearrange("(p t) o -> p (t o)", t=PACK))
+        nc.gpsimd.dma_start(out=w1_raw[:].bitcast(I32), in_=w1_words[0].bitcast(I32))
+        load_scale_rows([nc.scalar] * 4, xs_table, x_scales)
+        load_scale_rows([nc.gpsimd, nc.scalar, nc.scalar, nc.scalar], w1s_raw, w1_scales)
         make_identity(nc, ident[:])
+        nc.gpsimd.dma_start(out=unit_sb[:], in_=unit.rearrange("(p t) o -> p (t o)", t=PACK))
+        nc.gpsimd.memset(w2s_sb[:].bitcast(I32), 0)
         nc.gpsimd.dma_start(out=w2_sb[:].bitcast(I32), in_=w2_words[0].bitcast(I32))
         load_scale_rows([nc.gpsimd] * 4, w2s_sb, w2_scales)
 
         w1_dealt = sb("w1_dealt", [P, 2 * H], U8)
         w1s_dealt = sb("w1s_dealt", [P, H], U8)
         nc.vector.tensor_copy(
-            out=w1_dealt[:].rearrange("p (t m b) -> p m t b", t=PACK, b=2),
-            in_=w1_raw[:].rearrange("p (m t b) -> p m t b", t=PACK, b=2),
+            out=w1_dealt[:].rearrange("p (t m b) -> p t m b", t=PACK, b=2),
+            in_=w1_raw[:].rearrange("p (m t b) -> p t m b", t=PACK, b=2),
         )
         nc.vector.tensor_copy(
-            out=w1s_dealt[:].rearrange("p (t m) -> p m t", t=PACK),
-            in_=w1s_raw[:].rearrange("p (m t) -> p m t", t=PACK),
+            out=w1s_dealt[:].rearrange("p (t m) -> p t m", t=PACK),
+            in_=w1s_raw[:].rearrange("p (m t) -> p t m", t=PACK),
         )
 
         xs_picked = sb("xs_picked", [P, S], U8)
@@ -93,15 +94,14 @@ def tile_picked_ysembl_mul_p_kernel(
         for h in range(2):
             nc.vector.tensor_copy(x_picked[h], x_table[:].bitcast(U32).indirect(offs_sb[:, 32 * h : 32 * (h + 1)]))
 
-        late = sb("late", [P, 3 * S + U], F32, tag="x_table")
+        late = sb("late", [P, 3 * S + PACK * U], F32, tag="x_table")
         st_sb = [sb("st0", [P, S], F32, tag="w1_raw")] + [late[:, S * t : S * (t + 1)] for t in range(PACK - 1)]
-        mod_first = late[:, 3 * S :]
+        mod_sb = late[:, 3 * S :].rearrange("p (t r) -> p t r", t=PACK)
         for t in range(PACK):
             nc.sync.dma_start(out=st_sb[t][:, :], in_=st_rows[t])
-        nc.sync.dma_start(out=mod_first, in_=mod_rows[:, 0, :])
+        nc.sync.dma_start(out=late[:, 3 * S :], in_=mod.rearrange("(p t) r -> p (t r)", t=PACK))
 
         y_sb = [sb(f"y{t}", [P, S], F32) for t in range(PACK)]
-        flat = [[sb(f"flat{t}_{h}", [P, HALF], F32) for h in range(2)] for t in range(PACK)]
         sq = [[sb(f"sq{t}_{h}", [P, D, VB], F32) for h in range(2)] for t in range(PACK)]
         win = [sb(f"win{t}", [P, 3, V], F32) for t in range(PACK)]
         semb = [sb(f"semb{t}", [P, V], F32)[:, :] for t in range(PACK)]
@@ -132,24 +132,17 @@ def tile_picked_ysembl_mul_p_kernel(
         def moveout(t, h):
             if h == 0:
                 sums[t] = psum_sum.tile([P, 2, V], F32, name="sums")
+            flat = ring.tile([P, VB, D], F32, name="flat", align_bytes=64)
             nc.vector.tensor_tensor(
-                flat[t][h][:],
+                flat[:].rearrange("p v d -> p (v d)"),
                 y_sb[t][:].indirect(mv_sb[:, 32 * h : 32 * (h + 1)]),
                 st_sb[t][:, HALF * h : HALF * (h + 1)],
                 ALU.mult,
             )
-            nc.scalar.activation(
-                out=sq[t][h][:].rearrange("p d v -> p v d"),
-                in_=flat[t][h][:].rearrange("p (v d) -> p v d", d=D),
-                func=ACT.Square,
-            )
-            if t in PAIRED:
-                pairs = sb(f"pairs{t}_{h}", [P, VB, 2], F32)
-                groups = flat[t][h][:].rearrange("p (v d) -> p v d", d=D)
-                nc.vector.tensor_tensor(pairs[:], groups[:, :, 0:2], groups[:, :, 2:4], ALU.add)
-                terms = [pairs[:, :, e] for e in range(2)]
-            else:
-                terms = [flat[t][h][:, d::D] for d in range(D)]
+            nc.scalar.activation(out=sq[t][h][:].rearrange("p d v -> p v d"), in_=flat[:], func=ACT.Square)
+            pairs = sb(f"pairs{t}_{h}", [P, VB, 2], F32)
+            nc.vector.tensor_tensor(pairs[:], flat[:, :, 0:2], flat[:, :, 2:4], ALU.add)
+            terms = [pairs[:, :, e] for e in range(2)]
             cols = slice(VB * h, VB * (h + 1))
             for a, planes in enumerate((terms, [sq[t][h][:, d, :] for d in range(D)])):
                 for n, plane in enumerate(planes):
@@ -189,13 +182,11 @@ def tile_picked_ysembl_mul_p_kernel(
                 for r in range(2):
                     cols = slice(RH * r, RH * (r + 1))
                     nc.vector.scalar_tensor_tensor(
-                        hid32[r][:, t, :], mod_first[:, cols], neg_unit[:, t : t + 1], picked[t][:, cols],
+                        hid32[r][:, t, :], mod_sb[:, t, cols], neg_unit[:, t : t + 1], picked[t][:, cols],
                         ALU.mult, ALU.add,
                     )
 
-        nc.vector.tensor_scalar(neg_unit[:], unit_sb[:], -1.0, None, ALU.mult)
-        for t in FUSED:
-            nc.scalar.activation(out=picked[t][:], in_=mod_early[:, t - 1, :], func=ACT.Copy, scale=unit_sb[:, t : t + 1])
+        nc.scalar.activation(out=neg_unit[:], in_=unit_sb[:], func=ACT.Copy, scale=-1.0)
         first_product(0)
         first_product(1)
         moveout(0, 0)
@@ -204,12 +195,14 @@ def tile_picked_ysembl_mul_p_kernel(
         moveout(1, 0)
         first_product(3)
         moveout(1, 1)
-        for t in (2, 3):
-            for h in range(2):
-                moveout(t, h)
         for t in range(PACK):
             ratio(t)
             weighted(t)
+            if t + 2 < PACK:
+                moveout(t + 2, 0)
+                moveout(t + 2, 1)
+        for t in FUSED:
+            nc.scalar.activation(out=picked[t][:], in_=mod_sb[:, t, :], func=ACT.Copy, scale=unit_sb[:, t : t + 1])
         for t in range(PACK):
             output_times(t)
 
@@ -239,4 +232,4 @@ def tile_picked_ysembl_mul_p_kernel(
                     nc.vector.tensor_copy(out=result[:, b, :], in_=bank[:, :RH])
                 else:
                     nc.scalar.copy(out=result[:, b, :], in_=bank[:, :RH])
-            nc.sync.dma_start(out=out_rows[:, :, RH * r : RH * (r + 1)], in_=result[:])
+                nc.sync.dma_start(out=out_rows[:, b, RH * r : RH * (r + 1)], in_=result[:, b, :])

@@ -23,6 +23,7 @@ HALF = 512
 VB = 128
 RH = 256
 FUSED = (3,)
+VECTOR_LEVELS = (0, 0, 1, 2)
 
 
 def load_scale_rows(queues, plane, rows):
@@ -36,9 +37,8 @@ def tile_picked_ysembl_mul_p_kernel(
     nc = tc.nc
     with ExitStack() as ctx:
         keep = ctx.enter_context(tc.tile_pool(name="keep", bufs=1))
-        ring = ctx.enter_context(tc.tile_pool(name="ring", bufs=3))
         psum_y = ctx.enter_context(tc.psum_pool(name="psum_y", bufs=4))
-        psum_sum = ctx.enter_context(tc.psum_pool(name="psum_sum", bufs=4))
+        psum_sum = ctx.enter_context(tc.psum_pool(name="psum_sum", bufs=3))
 
         def sb(name, shape, dtype, tag=None):
             return keep.tile(shape, dtype, name=name, tag=tag or name, align_bytes=64)
@@ -51,9 +51,7 @@ def tile_picked_ysembl_mul_p_kernel(
         xs_table = sb("xs_table", [P, T], U8)
         w1_raw = sb("w1_raw", [P, 2 * H], U8)
         w1s_raw = sb("w1s_raw", [P, H], U8)
-        w2_sb = sb("w2_sb", [P, 2 * N], U8)
-        w2s_sb = sb("w2s_sb", [P, N], U8)
-        unit_sb = sb("unit_sb", [P, PACK], F32)
+        xs_rows = sb("xs_rows", [P, T], U8)
         ident = sb("ident", [P, P], F32)
 
         st_rows = st.rearrange("(p t) j -> t p j", t=PACK)
@@ -64,103 +62,123 @@ def tile_picked_ysembl_mul_p_kernel(
         nc.vector.memset(xs_table[:].bitcast(I32), 0)
         nc.vector.memset(w1s_raw[:].bitcast(I32), 0)
         nc.sync.dma_start(offs_sb[:], offs)
+        nc.sync.dma_start(out=w1_raw[:].bitcast(I32), in_=w1_words[0].bitcast(I32))
+        load_scale_rows([nc.sync] * 4, xs_rows, x_scales)
+        nc.sync.dma_start(out=x_table[:], in_=x_words[0].rearrange("p c r -> p (c r)").bitcast(I32))
         nc.sync.dma_start(mv_sb[:], mv)
         nc.sync.dma_start(out_t_sb[:], out_t)
-        nc.sync.dma_start(out=x_table[:], in_=x_words[0].rearrange("p c r -> p (c r)").bitcast(I32))
-        nc.gpsimd.dma_start(out=w1_raw[:].bitcast(I32), in_=w1_words[0].bitcast(I32))
-        load_scale_rows([nc.scalar] * 4, xs_table, x_scales)
-        load_scale_rows([nc.gpsimd, nc.scalar, nc.scalar, nc.scalar], w1s_raw, w1_scales)
+        load_scale_rows([nc.scalar] * 4, w1s_raw, w1_scales)
         make_identity(nc, ident[:])
-        nc.gpsimd.dma_start(out=unit_sb[:], in_=unit.rearrange("(p t) o -> p (t o)", t=PACK))
-        nc.gpsimd.memset(w2s_sb[:].bitcast(I32), 0)
-        nc.gpsimd.dma_start(out=w2_sb[:].bitcast(I32), in_=w2_words[0].bitcast(I32))
-        load_scale_rows([nc.gpsimd] * 4, w2s_sb, w2_scales)
 
-        w1_dealt = sb("w1_dealt", [P, 2 * H], U8)
+        def deal(dst, raw, pair, width):
+            nc.vector.tensor_copy(
+                out=dst[:].rearrange("p (t m b) -> p t m b", t=2, b=width),
+                in_=raw[:].rearrange("p (m t b) -> p t m b", t=PACK, b=width)[:, 2 * pair : 2 * pair + 2],
+            )
+
+        w1_dealt = [sb("w1_dealt0", [P, H], U8), sb("w1_dealt1", [P, H], U8, tag="x_table")]
         w1s_dealt = sb("w1s_dealt", [P, H], U8)
-        nc.vector.tensor_copy(
-            out=w1_dealt[:].rearrange("p (t m b) -> p t m b", t=PACK, b=2),
-            in_=w1_raw[:].rearrange("p (m t b) -> p t m b", t=PACK, b=2),
-        )
+        deal(w1_dealt[0], w1_raw, 0, 2)
+        for q in range(4):
+            rows = slice(32 * q, 32 * q + 4)
+            nc.vector.tensor_copy(out=xs_table[rows, :].bitcast(I32), in_=xs_rows[rows, :].bitcast(I32))
+
+        xs_picked = sb("xs_picked", [P, S], U8)
+        nc.vector.tensor_copy(xs_picked[:], xs_table[:].indirect(offs_sb[:]))
         nc.vector.tensor_copy(
             out=w1s_dealt[:].rearrange("p (t m) -> p t m", t=PACK),
             in_=w1s_raw[:].rearrange("p (m t) -> p t m", t=PACK),
         )
-
-        xs_picked = sb("xs_picked", [P, S], U8)
-        nc.vector.tensor_copy(xs_picked[:], xs_table[:].indirect(offs_sb[:]))
-        x_both = sb("x_picked", [P, S], U32, tag="xs_table")
-        x_picked = [x_both[:, HALF * h : HALF * (h + 1)] for h in range(2)]
+        x_picked = [sb(f"x_picked{h}", [P, HALF], U32, tag=tag) for h, tag in enumerate(("xs_table", "w1s_raw"))]
         for h in range(2):
-            nc.vector.tensor_copy(x_picked[h], x_table[:].bitcast(U32).indirect(offs_sb[:, 32 * h : 32 * (h + 1)]))
+            nc.vector.tensor_copy(x_picked[h][:], x_table[:].bitcast(U32).indirect(offs_sb[:, 32 * h : 32 * (h + 1)]))
+        deal(w1_dealt[1], w1_raw, 1, 2)
 
-        late = sb("late", [P, 3 * S + PACK * U], F32, tag="x_table")
-        st_sb = [sb("st0", [P, S], F32, tag="w1_raw")] + [late[:, S * t : S * (t + 1)] for t in range(PACK - 1)]
-        mod_sb = late[:, 3 * S :].rearrange("p (t r) -> p t r", t=PACK)
+        early = sb("early", [P, 2 * S], F32, tag="xs_rows")
+        late = sb("late", [P, 2 * S + PACK * U + PACK], F32, tag="w1_raw")
+        st_sb = [part[:, S * n : S * (n + 1)] for part in (early, late) for n in range(2)]
+        mod_flat = late[:, 2 * S : 2 * S + PACK * U]
+        mod_sb = mod_flat.rearrange("p (t r) -> p t r", t=PACK)
+        unit_sb = late[:, 2 * S + PACK * U :]
         for t in range(PACK):
-            nc.sync.dma_start(out=st_sb[t][:, :], in_=st_rows[t])
-        nc.sync.dma_start(out=late[:, 3 * S :], in_=mod.rearrange("(p t) r -> p (t r)", t=PACK))
+            nc.sync.dma_start(out=st_sb[t], in_=st_rows[t])
+        nc.sync.dma_start(out=unit_sb, in_=unit.rearrange("(p t) o -> p (t o)", t=PACK))
+        nc.sync.dma_start(out=mod_flat, in_=mod.rearrange("(p t) r -> p (t r)", t=PACK))
 
         y_sb = [sb(f"y{t}", [P, S], F32) for t in range(PACK)]
-        sq = [[sb(f"sq{t}_{h}", [P, D, VB], F32) for h in range(2)] for t in range(PACK)]
         win = [sb(f"win{t}", [P, 3, V], F32) for t in range(PACK)]
-        semb = [sb(f"semb{t}", [P, V], F32)[:, :] for t in range(PACK)]
-        rsq = [sb(f"rsq{t}", [P, V], F32)[:, :] for t in range(PACK)]
         picked = [sb(f"picked{t}", [P, U], F32) for t in range(PACK)]
         hid32 = [sb(f"hid32_{r}", [P, PACK, RH], F32) for r in range(2)]
         neg_unit = sb("neg_unit", [P, PACK], F32)
         sums = {}
 
         def first_product(t):
-            for h in range(2):
+            pieces = [(0, HALF), (HALF, HALF // 2), (HALF + HALF // 2, HALF // 2)] if t == 0 else [(0, HALF), (HALF, HALF)]
+            for n, (start, width) in enumerate(pieces):
+                cols = slice(start, start + width)
                 bank = psum_y.tile([P, HALF], F32, name="bank")
                 nc.tensor.matmul_mx(
-                    out=bank[:],
-                    lhsT=w1_dealt[:, 2 * P * t : 2 * P * (t + 1)].bitcast(FP4X4),
+                    out=bank[:, :width],
+                    lhsT=w1_dealt[t // 2][:, 2 * P * (t % 2) : 2 * P * (t % 2 + 1)].bitcast(FP4X4),
                     lhsT_scale=w1s_dealt[:, P * t : P * (t + 1)],
-                    rhs=x_picked[h].bitcast(FP8X4),
-                    rhs_scale=xs_picked[:, HALF * h : HALF * (h + 1)],
+                    rhs=x_picked[start // HALF][:, start % HALF : start % HALF + width].bitcast(FP8X4),
+                    rhs_scale=xs_picked[:, cols],
                     start=True,
                     stop=True,
                 )
-                dst = y_sb[t][:, HALF * h : HALF * (h + 1)]
-                if t == 0 and h == 1:
-                    nc.vector.tensor_copy(out=dst, in_=bank[:])
-                else:
-                    nc.scalar.copy(out=dst, in_=bank[:])
+                copy = nc.vector.tensor_copy if n == 2 else nc.scalar.copy
+                copy(out=y_sb[t][:, cols], in_=bank[:, :width])
 
         def moveout(t, h):
-            if h == 0:
-                sums[t] = psum_sum.tile([P, 2, V], F32, name="sums")
-            flat = ring.tile([P, VB, D], F32, name="flat", align_bytes=64)
+            levels = VECTOR_LEVELS[t]
+            cols = slice(VB * h, VB * (h + 1))
+            both = sb(f"both{t}_{h}", [P, 2 if levels == 2 else 1, HALF], F32)
+            flat = both[:, 0, :].rearrange("p (v d) -> p v d", d=D)
             nc.vector.tensor_tensor(
-                flat[:].rearrange("p v d -> p (v d)"),
+                both[:, 0, :],
                 y_sb[t][:].indirect(mv_sb[:, 32 * h : 32 * (h + 1)]),
                 st_sb[t][:, HALF * h : HALF * (h + 1)],
                 ALU.mult,
             )
-            nc.scalar.activation(out=sq[t][h][:].rearrange("p d v -> p v d"), in_=flat[:], func=ACT.Square)
-            pairs = sb(f"pairs{t}_{h}", [P, VB, 2], F32)
-            nc.vector.tensor_tensor(pairs[:], flat[:, :, 0:2], flat[:, :, 2:4], ALU.add)
-            terms = [pairs[:, :, e] for e in range(2)]
-            cols = slice(VB * h, VB * (h + 1))
-            for a, planes in enumerate((terms, [sq[t][h][:, d, :] for d in range(D)])):
+            if levels == 2:
+                sums[t] = win[t][:, 1:, :]
+                nc.scalar.activation(out=both[:, 1, :], in_=both[:, 0, :], func=ACT.Square)
+                groups = both[:].rearrange("p a (v d) -> p (a v) d", d=D)
+                pairs = sb(f"pairs{t}_{h}", [P, 2, VB, 2], F32)
+                nc.vector.tensor_tensor(
+                    pairs[:].rearrange("p a v e -> p (a v) e"), groups[:, :, 0:2], groups[:, :, 2:4], ALU.add
+                )
+                nc.vector.tensor_tensor(sums[t][:, :, cols], pairs[:, :, :, 0], pairs[:, :, :, 1], ALU.add)
+                return
+            if h == 0:
+                sums[t] = psum_sum.tile([P, 2, V], F32, name="sums")
+            squares = sb(f"squares{t}_{h}", [P, D, VB], F32)
+            nc.scalar.activation(out=squares[:].rearrange("p d v -> p v d"), in_=flat, func=ACT.Square)
+            if levels == 1:
+                pairs = sb(f"pairs{t}_{h}", [P, VB, 2], F32)
+                nc.vector.tensor_tensor(pairs[:], flat[:, :, 0:2], flat[:, :, 2:4], ALU.add)
+                terms = [pairs[:, :, e] for e in range(2)]
+            else:
+                terms = [flat[:, :, d] for d in range(D)]
+            for a, planes in enumerate((terms, [squares[:, d, :] for d in range(D)])):
                 for n, plane in enumerate(planes):
                     nc.tensor.matmul(
                         sums[t][:, a, cols], lhsT=plane, rhs=ident[:],
                         start=(n == 0), stop=(n == len(planes) - 1), is_transpose=True,
                     )
 
-        def ratio(t):
+        def semblance(t):
             stack, energ = sums[t][:, 0, :], sums[t][:, 1, :]
-            rs, q = rsq[t], win[t][:, 1, :]
-            nc.scalar.activation(out=rs, in_=energ, func=ACT.Abs_reciprocal_sqrt, scale=4.0, bias=0.5)
-            nc.vector.tensor_tensor(q, stack, rs, ALU.mult)
-
-        def weighted(t):
-            stack, q, w = sums[t][:, 0, :], win[t][:, 1, :], win[t][:, 2, :]
-            nc.scalar.activation(out=semb[t], in_=q, func=ACT.Square)
-            nc.vector.tensor_tensor(w, stack, semb[t], ALU.mult)
+            turned = VECTOR_LEVELS[t] < 2
+            rs, semb = sb(f"rs{t}", [P, V], F32), sb(f"semb{t}", [P, V], F32)
+            q = win[t][:, 1, :] if turned else sb(f"q{t}", [P, V], F32)[:, :]
+            nc.scalar.activation(out=rs[:], in_=energ, func=ACT.Abs_reciprocal_sqrt, scale=4.0, bias=0.5)
+            nc.vector.tensor_tensor(q, stack, rs[:], ALU.mult)
+            nc.scalar.activation(out=semb[:], in_=q, func=ACT.Square)
+            if not turned:
+                nc.vector.scalar_tensor_tensor(win[t][:, 0, :], stack, unit_sb[:, t : t + 1], semb[:], ALU.mult, ALU.mult)
+                return
+            nc.vector.tensor_tensor(win[t][:, 2, :], stack, semb[:], ALU.mult)
             back = psum_y.tile([P, HALF], F32, name="bank")
             for h in range(2):
                 cols = slice(VB * h, VB * (h + 1))
@@ -186,7 +204,7 @@ def tile_picked_ysembl_mul_p_kernel(
                         ALU.mult, ALU.add,
                     )
 
-        nc.scalar.activation(out=neg_unit[:], in_=unit_sb[:], func=ACT.Copy, scale=-1.0)
+        nc.scalar.activation(out=neg_unit[:], in_=unit_sb, func=ACT.Copy, scale=-1.0)
         first_product(0)
         first_product(1)
         moveout(0, 0)
@@ -195,9 +213,13 @@ def tile_picked_ysembl_mul_p_kernel(
         moveout(1, 0)
         first_product(3)
         moveout(1, 1)
+        w2_sb = sb("w2_sb", [P, 2 * N], U8, tag="xs_table")
+        w2s_sb = sb("w2s_sb", [P, N], U8, tag="w1s_raw")
+        nc.sync.dma_start(out=w2_sb[:].bitcast(I32), in_=w2_words[0].bitcast(I32))
+        nc.gpsimd.memset(w2s_sb[:].bitcast(I32), 0)
+        load_scale_rows([nc.sync] * 4, w2s_sb, w2_scales)
         for t in range(PACK):
-            ratio(t)
-            weighted(t)
+            semblance(t)
             if t + 2 < PACK:
                 moveout(t + 2, 0)
                 moveout(t + 2, 1)

@@ -22,8 +22,9 @@ PACK = 4
 HALF = 512
 VB = 128
 RH = 256
-FUSED = (3,)
-VECTOR_LEVELS = (0, 0, 1, 2)
+FUSED = (0, 3)
+VECTOR_LEVELS = (0, 0, 0, 2)
+SCALAR_HALF = (2, 1)
 
 
 def load_scale_rows(queues, plane, rows):
@@ -55,19 +56,19 @@ def tile_picked_ysembl_mul_p_kernel(
         ident = sb("ident", [P, P], F32)
 
         st_rows = st.rearrange("(p t) j -> t p j", t=PACK)
+        nc.vector.memset(xs_table[:].bitcast(I32), 0)
+        nc.vector.memset(w1s_raw[:].bitcast(I32), 0)
+        nc.sync.dma_start(offs_sb[:], offs)
+        load_scale_rows([nc.scalar, nc.scalar, nc.sync, nc.sync], xs_rows, x_scales)
+        nc.scalar.dma_start(out=w1_raw[:].bitcast(I32), in_=w1_words[0].bitcast(I32))
+        nc.scalar.dma_start(out=x_table[:], in_=x_words[0].rearrange("p c r -> p (c r)").bitcast(I32))
+        nc.sync.dma_start(mv_sb[:], mv)
+        nc.sync.dma_start(out_t_sb[:], out_t)
+        load_scale_rows([nc.sync] * 4, w1s_raw, w1_scales)
         warm = sb("warm", [P, 2], F32)
         nc.gpsimd.memset(warm[:, 0:1], 1.0)
         nc.scalar.activation(out=warm[:, 1:2], in_=warm[:, 0:1], func=ACT.Abs_reciprocal_sqrt, scale=4.0, bias=0.5)
 
-        nc.vector.memset(xs_table[:].bitcast(I32), 0)
-        nc.vector.memset(w1s_raw[:].bitcast(I32), 0)
-        nc.sync.dma_start(offs_sb[:], offs)
-        nc.sync.dma_start(out=w1_raw[:].bitcast(I32), in_=w1_words[0].bitcast(I32))
-        load_scale_rows([nc.sync] * 4, xs_rows, x_scales)
-        nc.sync.dma_start(out=x_table[:], in_=x_words[0].rearrange("p c r -> p (c r)").bitcast(I32))
-        nc.sync.dma_start(mv_sb[:], mv)
-        nc.sync.dma_start(out_t_sb[:], out_t)
-        load_scale_rows([nc.scalar] * 4, w1s_raw, w1_scales)
         make_identity(nc, ident[:])
 
         def deal(dst, raw, pair, width):
@@ -78,10 +79,10 @@ def tile_picked_ysembl_mul_p_kernel(
 
         w1_dealt = [sb("w1_dealt0", [P, H], U8), sb("w1_dealt1", [P, H], U8, tag="x_table")]
         w1s_dealt = sb("w1s_dealt", [P, H], U8)
-        deal(w1_dealt[0], w1_raw, 0, 2)
         for q in range(4):
             rows = slice(32 * q, 32 * q + 4)
             nc.vector.tensor_copy(out=xs_table[rows, :].bitcast(I32), in_=xs_rows[rows, :].bitcast(I32))
+        deal(w1_dealt[0], w1_raw, 0, 2)
 
         xs_picked = sb("xs_picked", [P, S], U8)
         nc.vector.tensor_copy(xs_picked[:], xs_table[:].indirect(offs_sb[:]))
@@ -134,12 +135,12 @@ def tile_picked_ysembl_mul_p_kernel(
             cols = slice(VB * h, VB * (h + 1))
             both = sb(f"both{t}_{h}", [P, 2 if levels == 2 else 1, HALF], F32)
             flat = both[:, 0, :].rearrange("p (v d) -> p v d", d=D)
-            nc.vector.tensor_tensor(
-                both[:, 0, :],
-                y_sb[t][:].indirect(mv_sb[:, 32 * h : 32 * (h + 1)]),
-                st_sb[t][:, HALF * h : HALF * (h + 1)],
-                ALU.mult,
-            )
+            moved = y_sb[t][:].indirect(mv_sb[:, 32 * h : 32 * (h + 1)])
+            if (t, h) == SCALAR_HALF:
+                fetched = sb("fetched", [P, HALF], F32)
+                nc.scalar.activation(fetched[:], moved, ACT.Copy)
+                moved = fetched[:]
+            nc.vector.tensor_tensor(both[:, 0, :], moved, st_sb[t][:, HALF * h : HALF * (h + 1)], ALU.mult)
             if levels == 2:
                 sums[t] = win[t][:, 1:, :]
                 nc.scalar.activation(out=both[:, 1, :], in_=both[:, 0, :], func=ACT.Square)
@@ -167,23 +168,30 @@ def tile_picked_ysembl_mul_p_kernel(
                         start=(n == 0), stop=(n == len(planes) - 1), is_transpose=True,
                     )
 
-        def semblance(t):
-            stack, energ = sums[t][:, 0, :], sums[t][:, 1, :]
-            turned = VECTOR_LEVELS[t] < 2
-            rs, semb = sb(f"rs{t}", [P, V], F32), sb(f"semb{t}", [P, V], F32)
-            q = win[t][:, 1, :] if turned else sb(f"q{t}", [P, V], F32)[:, :]
-            nc.scalar.activation(out=rs[:], in_=energ, func=ACT.Abs_reciprocal_sqrt, scale=4.0, bias=0.5)
-            nc.vector.tensor_tensor(q, stack, rs[:], ALU.mult)
-            nc.scalar.activation(out=semb[:], in_=q, func=ACT.Square)
-            if not turned:
-                nc.vector.scalar_tensor_tensor(win[t][:, 0, :], stack, unit_sb[:, t : t + 1], semb[:], ALU.mult, ALU.mult)
-                return
-            nc.vector.tensor_tensor(win[t][:, 2, :], stack, semb[:], ALU.mult)
-            back = psum_y.tile([P, HALF], F32, name="bank")
-            for h in range(2):
-                cols = slice(VB * h, VB * (h + 1))
-                nc.tensor.transpose(back[:, cols], win[t][:, 2, cols], ident[:])
-            nc.scalar.activation(out=win[t][:, 0, :], in_=back[:, :V], func=ACT.Copy, scale=unit_sb[:, t : t + 1])
+        rs = [sb(f"rs{t}", [P, V], F32) for t in range(PACK)]
+        semb = [sb(f"semb{t}", [P, V], F32) for t in range(PACK)]
+        ratio = [win[t][:, 1, :] if VECTOR_LEVELS[t] < 2 else sb(f"q{t}", [P, V], F32)[:, :] for t in range(PACK)]
+
+        def semblance():
+            for t in range(PACK):
+                nc.scalar.activation(out=rs[t][:], in_=sums[t][:, 1, :], func=ACT.Abs_reciprocal_sqrt, scale=4.0, bias=0.5)
+            for t in range(PACK):
+                nc.vector.tensor_tensor(ratio[t], sums[t][:, 0, :], rs[t][:], ALU.mult)
+            for t in range(PACK):
+                nc.scalar.activation(out=semb[t][:], in_=ratio[t], func=ACT.Square)
+            for t in range(PACK):
+                stack = sums[t][:, 0, :]
+                if VECTOR_LEVELS[t] == 2:
+                    nc.vector.scalar_tensor_tensor(
+                        win[t][:, 0, :], stack, unit_sb[:, t : t + 1], semb[t][:], ALU.mult, ALU.mult
+                    )
+                    continue
+                nc.vector.tensor_tensor(win[t][:, 2, :], stack, semb[t][:], ALU.mult)
+                back = psum_y.tile([P, HALF], F32, name="bank")
+                for h in range(2):
+                    cols = slice(VB * h, VB * (h + 1))
+                    nc.tensor.transpose(back[:, cols], win[t][:, 2, cols], ident[:])
+                nc.scalar.activation(out=win[t][:, 0, :], in_=back[:, :V], func=ACT.Copy, scale=unit_sb[:, t : t + 1])
 
         def output_times(t):
             window = win[t][:].rearrange("p a v -> p (a v)")
@@ -218,11 +226,10 @@ def tile_picked_ysembl_mul_p_kernel(
         nc.sync.dma_start(out=w2_sb[:].bitcast(I32), in_=w2_words[0].bitcast(I32))
         nc.gpsimd.memset(w2s_sb[:].bitcast(I32), 0)
         load_scale_rows([nc.sync] * 4, w2s_sb, w2_scales)
-        for t in range(PACK):
-            semblance(t)
-            if t + 2 < PACK:
-                moveout(t + 2, 0)
-                moveout(t + 2, 1)
+        for t in (2, 3):
+            for h in range(2):
+                moveout(t, h)
+        semblance()
         for t in FUSED:
             nc.scalar.activation(out=picked[t][:], in_=mod_sb[:, t, :], func=ACT.Copy, scale=unit_sb[:, t : t + 1])
         for t in range(PACK):

from contextlib import ExitStack

import concourse.mybir as mybir
from concourse.masks import make_identity

K, T, S, D, N, H, V, U = 512, 4096, 1024, 4, 256, 512, 256, 512
FLOPS = 2 * K * H * S + 2 * H * N * U

F32 = mybir.dt.float32
BF16 = mybir.dt.bfloat16
I32 = mybir.dt.int32
U32 = mybir.dt.uint32
U16 = mybir.dt.uint16
U8 = mybir.dt.uint8
FP8X4 = mybir.dt.float8_e4m3fn_x4
FP4X4 = mybir.dt.float4_e2m1fn_x4
ALU = mybir.AluOpType
ACT = mybir.ActivationFunctionType

P = 128
PACK = 4
HALF = 512
VB = 128
RH = 256
FUSED = (0, 3)
VECTOR_LEVELS = (0, 0, 0, 2)
SCALAR_HALF = (2, 1)


def load_scale_rows(queues, plane, rows):
    for q, queue in enumerate(queues):
        queue.dma_start(out=plane[32 * q : 32 * q + 4, :].bitcast(I32), in_=rows[0, 4 * q : 4 * q + 4, :].bitcast(I32))


def tile_picked_ysembl_mul_p_kernel(
    tc, x_words, x_scales, w1_words, w1_scales, st, mod, unit, w2_words, w2_scales, offs, mv, out_t, out
):
    nc = tc.nc
    with ExitStack() as ctx:
        keep = ctx.enter_context(tc.tile_pool(name="keep", bufs=1))
        psum_y = ctx.enter_context(tc.psum_pool(name="psum_y", bufs=4))
        psum_sum = ctx.enter_context(tc.psum_pool(name="psum_sum", bufs=3))

        def sb(name, shape, dtype, tag=None):
            return keep.tile(shape, dtype, name=name, tag=tag or name, align_bytes=64)

        offs_sb = keep.tile([P, S // 16], U16, name="offs_sb")
        mv_sb = keep.tile([P, S // 16], U16, name="mv_sb")
        out_t_sb = keep.tile([P, U // 16], U16, name="out_t_sb")

        x_table = sb("x_table", [P, T], I32)
        xs_table = sb("xs_table", [P, T], U8)
        w1_raw = sb("w1_raw", [P, 2 * H], U8)
        w1s_raw = sb("w1s_raw", [P, H], U8)
        xs_rows = sb("xs_rows", [P, T], U8)
        ident = sb("ident", [P, P], F32)

        st_rows = st.rearrange("(p t) j -> t p j", t=PACK)
        nc.vector.memset(xs_table[:].bitcast(I32), 0)
        nc.vector.memset(w1s_raw[:].bitcast(I32), 0)
        nc.sync.dma_start(offs_sb[:], offs)
        load_scale_rows([nc.scalar, nc.scalar, nc.sync, nc.sync], xs_rows, x_scales)
        nc.scalar.dma_start(out=w1_raw[:].bitcast(I32), in_=w1_words[0].bitcast(I32))
        nc.scalar.dma_start(out=x_table[:], in_=x_words[0].rearrange("p c r -> p (c r)").bitcast(I32))
        nc.sync.dma_start(mv_sb[:], mv)
        nc.sync.dma_start(out_t_sb[:], out_t)
        load_scale_rows([nc.sync] * 4, w1s_raw, w1_scales)
        warm = sb("warm", [P, 2], F32)
        nc.gpsimd.memset(warm[:, 0:1], 1.0)
        nc.scalar.activation(out=warm[:, 1:2], in_=warm[:, 0:1], func=ACT.Abs_reciprocal_sqrt, scale=4.0, bias=0.5)

        make_identity(nc, ident[:])

        def deal(dst, raw, pair, width):
            nc.vector.tensor_copy(
                out=dst[:].rearrange("p (t m b) -> p t m b", t=2, b=width),
                in_=raw[:].rearrange("p (m t b) -> p t m b", t=PACK, b=width)[:, 2 * pair : 2 * pair + 2],
            )

        w1_dealt = [sb("w1_dealt0", [P, H], U8), sb("w1_dealt1", [P, H], U8, tag="x_table")]
        w1s_dealt = sb("w1s_dealt", [P, H], U8)
        for q in range(4):
            rows = slice(32 * q, 32 * q + 4)
            nc.vector.tensor_copy(out=xs_table[rows, :].bitcast(I32), in_=xs_rows[rows, :].bitcast(I32))
        deal(w1_dealt[0], w1_raw, 0, 2)

        xs_picked = sb("xs_picked", [P, S], U8)
        nc.vector.tensor_copy(xs_picked[:], xs_table[:].indirect(offs_sb[:]))
        nc.vector.tensor_copy(
            out=w1s_dealt[:].rearrange("p (t m) -> p t m", t=PACK),
            in_=w1s_raw[:].rearrange("p (m t) -> p t m", t=PACK),
        )
        x_picked = [sb(f"x_picked{h}", [P, HALF], U32, tag=tag) for h, tag in enumerate(("xs_table", "w1s_raw"))]
        for h in range(2):
            nc.vector.tensor_copy(x_picked[h][:], x_table[:].bitcast(U32).indirect(offs_sb[:, 32 * h : 32 * (h + 1)]))
        deal(w1_dealt[1], w1_raw, 1, 2)

        early = sb("early", [P, 2 * S], F32, tag="xs_rows")
        late = sb("late", [P, 2 * S + PACK * U + PACK], F32, tag="w1_raw")
        st_sb = [part[:, S * n : S * (n + 1)] for part in (early, late) for n in range(2)]
        mod_flat = late[:, 2 * S : 2 * S + PACK * U]
        mod_sb = mod_flat.rearrange("p (t r) -> p t r", t=PACK)
        unit_sb = late[:, 2 * S + PACK * U :]
        for t in range(PACK):
            nc.sync.dma_start(out=st_sb[t], in_=st_rows[t])
        nc.sync.dma_start(out=unit_sb, in_=unit.rearrange("(p t) o -> p (t o)", t=PACK))
        nc.sync.dma_start(out=mod_flat, in_=mod.rearrange("(p t) r -> p (t r)", t=PACK))

        y_sb = [sb(f"y{t}", [P, S], F32) for t in range(PACK)]
        win = [sb(f"win{t}", [P, 3, V], F32) for t in range(PACK)]
        picked = [sb(f"picked{t}", [P, U], F32) for t in range(PACK)]
        hid32 = [sb(f"hid32_{r}", [P, PACK, RH], F32) for r in range(2)]
        neg_unit = sb("neg_unit", [P, PACK], F32)
        sums = {}

        def first_product(t):
            pieces = [(0, HALF), (HALF, HALF // 2), (HALF + HALF // 2, HALF // 2)] if t == 0 else [(0, HALF), (HALF, HALF)]
            for n, (start, width) in enumerate(pieces):
                cols = slice(start, start + width)
                bank = psum_y.tile([P, HALF], F32, name="bank")
                nc.tensor.matmul_mx(
                    out=bank[:, :width],
                    lhsT=w1_dealt[t // 2][:, 2 * P * (t % 2) : 2 * P * (t % 2 + 1)].bitcast(FP4X4),
                    lhsT_scale=w1s_dealt[:, P * t : P * (t + 1)],
                    rhs=x_picked[start // HALF][:, start % HALF : start % HALF + width].bitcast(FP8X4),
                    rhs_scale=xs_picked[:, cols],
                    start=True,
                    stop=True,
                )
                copy = nc.vector.tensor_copy if n == 2 else nc.scalar.copy
                copy(out=y_sb[t][:, cols], in_=bank[:, :width])

        def moveout(t, h):
            levels = VECTOR_LEVELS[t]
            cols = slice(VB * h, VB * (h + 1))
            both = sb(f"both{t}_{h}", [P, 2 if levels == 2 else 1, HALF], F32)
            flat = both[:, 0, :].rearrange("p (v d) -> p v d", d=D)
            moved = y_sb[t][:].indirect(mv_sb[:, 32 * h : 32 * (h + 1)])
            if (t, h) == SCALAR_HALF:
                fetched = sb("fetched", [P, HALF], F32)
                nc.scalar.activation(fetched[:], moved, ACT.Copy)
                moved = fetched[:]
            nc.vector.tensor_tensor(both[:, 0, :], moved, st_sb[t][:, HALF * h : HALF * (h + 1)], ALU.mult)
            if levels == 2:
                sums[t] = win[t][:, 1:, :]
                nc.scalar.activation(out=both[:, 1, :], in_=both[:, 0, :], func=ACT.Square)
                groups = both[:].rearrange("p a (v d) -> p (a v) d", d=D)
                pairs = sb(f"pairs{t}_{h}", [P, 2, VB, 2], F32)
                nc.vector.tensor_tensor(
                    pairs[:].rearrange("p a v e -> p (a v) e"), groups[:, :, 0:2], groups[:, :, 2:4], ALU.add
                )
                nc.vector.tensor_tensor(sums[t][:, :, cols], pairs[:, :, :, 0], pairs[:, :, :, 1], ALU.add)
                return
            if h == 0:
                sums[t] = psum_sum.tile([P, 2, V], F32, name="sums")
            squares = sb(f"squares{t}_{h}", [P, D, VB], F32)
            nc.scalar.activation(out=squares[:].rearrange("p d v -> p v d"), in_=flat, func=ACT.Square)
            if levels == 1:
                pairs = sb(f"pairs{t}_{h}", [P, VB, 2], F32)
                nc.vector.tensor_tensor(pairs[:], flat[:, :, 0:2], flat[:, :, 2:4], ALU.add)
                terms = [pairs[:, :, e] for e in range(2)]
            else:
                terms = [flat[:, :, d] for d in range(D)]
            for a, planes in enumerate((terms, [squares[:, d, :] for d in range(D)])):
                for n, plane in enumerate(planes):
                    nc.tensor.matmul(
                        sums[t][:, a, cols], lhsT=plane, rhs=ident[:],
                        start=(n == 0), stop=(n == len(planes) - 1), is_transpose=True,
                    )

        rs = [sb(f"rs{t}", [P, V], F32) for t in range(PACK)]
        semb = [sb(f"semb{t}", [P, V], F32) for t in range(PACK)]
        ratio = [win[t][:, 1, :] if VECTOR_LEVELS[t] < 2 else sb(f"q{t}", [P, V], F32)[:, :] for t in range(PACK)]

        def semblance():
            for t in range(PACK):
                nc.scalar.activation(out=rs[t][:], in_=sums[t][:, 1, :], func=ACT.Abs_reciprocal_sqrt, scale=4.0, bias=0.5)
            for t in range(PACK):
                nc.vector.tensor_tensor(ratio[t], sums[t][:, 0, :], rs[t][:], ALU.mult)
            for t in range(PACK):
                nc.scalar.activation(out=semb[t][:], in_=ratio[t], func=ACT.Square)
            for t in range(PACK):
                stack = sums[t][:, 0, :]
                if VECTOR_LEVELS[t] == 2:
                    nc.vector.scalar_tensor_tensor(
                        win[t][:, 0, :], stack, unit_sb[:, t : t + 1], semb[t][:], ALU.mult, ALU.mult
                    )
                    continue
                nc.vector.tensor_tensor(win[t][:, 2, :], stack, semb[t][:], ALU.mult)
                back = psum_y.tile([P, HALF], F32, name="bank")
                for h in range(2):
                    cols = slice(VB * h, VB * (h + 1))
                    nc.tensor.transpose(back[:, cols], win[t][:, 2, cols], ident[:])
                nc.scalar.activation(out=win[t][:, 0, :], in_=back[:, :V], func=ACT.Copy, scale=unit_sb[:, t : t + 1])

        def output_times(t):
            window = win[t][:].rearrange("p a v -> p (a v)")
            if t in FUSED:
                for r in range(2):
                    nc.vector.tensor_tensor(
                        hid32[r][:, t, :],
                        window.indirect(out_t_sb[:, 16 * r : 16 * (r + 1)]),
                        picked[t][:, RH * r : RH * (r + 1)],
                        ALU.subtract,
                    )
            else:
                nc.scalar.activation(picked[t][:], window.indirect(out_t_sb[:]), ACT.Copy)
                for r in range(2):
                    cols = slice(RH * r, RH * (r + 1))
                    nc.vector.scalar_tensor_tensor(
                        hid32[r][:, t, :], mod_sb[:, t, cols], neg_unit[:, t : t + 1], picked[t][:, cols],
                        ALU.mult, ALU.add,
                    )

        nc.scalar.activation(out=neg_unit[:], in_=unit_sb, func=ACT.Copy, scale=-1.0)
        first_product(0)
        first_product(1)
        moveout(0, 0)
        moveout(0, 1)
        first_product(2)
        moveout(1, 0)
        first_product(3)
        moveout(1, 1)
        w2_sb = sb("w2_sb", [P, 2 * N], U8, tag="xs_table")
        w2s_sb = sb("w2s_sb", [P, N], U8, tag="w1s_raw")
        nc.sync.dma_start(out=w2_sb[:].bitcast(I32), in_=w2_words[0].bitcast(I32))
        nc.gpsimd.memset(w2s_sb[:].bitcast(I32), 0)
        load_scale_rows([nc.sync] * 4, w2s_sb, w2_scales)
        for t in (2, 3):
            for h in range(2):
                moveout(t, h)
        semblance()
        for t in FUSED:
            nc.scalar.activation(out=picked[t][:], in_=mod_sb[:, t, :], func=ACT.Copy, scale=unit_sb[:, t : t + 1])
        for t in range(PACK):
            output_times(t)

        out_rows = out.rearrange("(b p) r -> p b r", p=P)
        for r in range(2):
            hid = sb(f"hid{r}", [P, RH, PACK], BF16)
            (nc.scalar.copy if r == 0 else nc.vector.tensor_copy)(
                out=hid[:].rearrange("p (c i) t -> p c t i", i=4),
                in_=hid32[r][:].rearrange("p t (c i) -> p c t i", i=4),
            )
            codes = sb(f"codes{r}", [P, RH], U32)
            scales = sb(f"scales{r}", [P, RH], U8)
            nc.vector.quantize_mx(out=codes[:].bitcast(FP8X4), scales=scales[:], in_=hid[:].rearrange("p r t -> p (r t)"))
            result = sb(f"result{r}", [P, N // P, RH], F32)
            for b in range(N // P):
                bank = psum_y.tile([P, HALF], F32, name="bank")
                nc.tensor.matmul_mx(
                    out=bank[:, :RH],
                    lhsT=w2_sb[:, 2 * P * b : 2 * P * (b + 1)].bitcast(FP4X4),
                    lhsT_scale=w2s_sb[:, P * b : P * (b + 1)],
                    rhs=codes[:].bitcast(FP8X4),
                    rhs_scale=scales[:],
                    start=True,
                    stop=True,
                )
                if r == 1 and b == 1:
                    nc.vector.tensor_copy(out=result[:, b, :], in_=bank[:, :RH])
                else:
                    nc.scalar.copy(out=result[:, b, :], in_=bank[:, :RH])
                nc.sync.dma_start(out=out_rows[:, b, RH * r : RH * (r + 1)], in_=result[:, b, :])
